import numpy as np
import ml_dtypes


def mxq(x, axis, fmt="e4m3"):
    dtype, down = {"e4m3": (ml_dtypes.float8_e4m3fn, 7), "e5m2": (ml_dtypes.float8_e5m2, 14)}[fmt]
    v = np.moveaxis(np.asarray(x, np.float32).astype(ml_dtypes.bfloat16).astype(np.float64), axis, -1)
    blocks = v.reshape(v.shape[:-1] + (-1, 32))
    amax = np.abs(blocks).max(-1, keepdims=True)
    byte = np.maximum(np.where(amax > 0, np.frexp(amax)[1] - 1 + 127, 0) - down, 1)
    scale = np.exp2(byte - 127.0)
    codes = (blocks / scale).astype(np.float32).astype(dtype).astype(np.float64)
    return np.moveaxis((codes * scale).reshape(v.shape), -1, axis)


WIDE = False


def mx_kscale(k):
    if not WIDE:
        return np.ones(k)
    levels = np.array([10, -10, 5, -5, 0])
    if k % 512:
        return np.exp2(np.random.permutation(np.resize(levels, k // 32))).repeat(32)
    a = np.empty((k // 512, 16))
    for p in range(k // 512):
        a[p, :8] = np.random.permutation(np.resize(levels, 8))
        for g in range(8):
            far = levels[np.abs(levels - a[p, g]) >= 10]
            a[p, g + 8] = far[np.random.randint(len(far))]
    return np.exp2(a.ravel()).repeat(32)


def f64(x):
    return np.asarray(x).astype(np.float64)


def striped(idx):
    return np.tile(idx.reshape(-1, 16).T, (8, 1)).astype(np.uint16)


def unstriped(offs):
    return offs[:16].T.reshape(-1).astype(np.int64)


def striped8(idx):
    return np.concatenate([x.reshape(-1, 16).T for x in idx]).astype(np.uint16)


def runs(offs, k):
    lists = np.stack([offs[16 * r : 16 * r + 16].T.reshape(-1) for r in range(8)]).astype(np.int64)
    return lists[np.arange(k) % 512 // 64]


def pack_weight(w):
    k, n = w.shape
    w = f64(np.asarray(w, np.float32).astype(ml_dtypes.bfloat16)).reshape(k // 32, 32, n)
    amax = np.abs(w).max(1)
    byte = np.clip(np.where(amax > 0, np.frexp(amax)[1] - 1 + 127 - 7, 1), 1, 254)
    scaled = (w * np.exp2(127.0 - byte)[:, None, :]).reshape(k, n).astype(np.float32)
    words = np.ascontiguousarray(scaled.reshape(k // 512, 128, 4, n).transpose(0, 1, 3, 2)).astype(ml_dtypes.float8_e4m3fn).view(np.uint8)
    return words, np.ascontiguousarray(byte.astype(np.uint8).reshape(k // 512, 16, n))


def unpack_weight(words, scales):
    g, p, n, _ = words.shape
    vals = np.ascontiguousarray(words).view(ml_dtypes.float8_e4m3fn).astype(np.float64) * np.repeat(np.exp2(scales.astype(np.float64) - 127.0), 8, axis=1)[..., None]
    return vals.transpose(0, 1, 3, 2).reshape(g * 512, n)


K, T, S, H, W, C, J = 512, 2048, 512, 512, 2048, 512, 512


def setup_inputs():
    n = np.random.standard_normal
    s = mx_kscale(K)[:, None]
    packed_xT = pack_weight(n((K, T)) * s)
    return {
        "x_words": packed_xT[0],
        "x_scales": packed_xT[1],
        "w1": (n((K, H)) / np.sqrt(K) / s).astype(np.float32),
        "tau": np.random.uniform(0.3, 0.9, (H, 1)).astype(np.float32),
        "gs": (np.random.uniform(0.5, 1.5, (K, 1)) / s).astype(np.float32),
        "tab": n((C, J)).astype(np.float32),
        "offs": striped8(np.random.randint(0, T, (8, S))),
        "n1": striped(np.random.randint(0, S, W)),
        "cand": striped8(np.random.randint(0, T, (8, C))),
        "n2": striped(np.random.randint(0, J, S)),
        "n3": striped(np.random.randint(0, J, S)),
        "n4": striped(np.random.permutation(S)),
    }


def reference(x_words, x_scales, w1, tau, gs, tab, offs, n1, cand, n2, n3, n4):
    x_cand = unpack_weight(x_words, x_scales)[np.arange(K)[:, None], runs(cand, K)]
    xq = unpack_weight(x_words, x_scales)[np.arange(K)[:, None], runs(offs, K)]
    y = mxq(f64(w1), 0, "e4m3").T @ xq
    top = y.max(axis=1, keepdims=True)
    ea = np.exp(f64(tau) * (y[:, unstriped(n1)] - top))
    mx = ea.reshape(H, S, 4).max(axis=2)
    mn = ea.reshape(H, S, 4).min(axis=2)
    z = f64(gs) * (3.0 * (y * (mx - mn)))
    s = 0.0625 * ((x_cand.T @ mxq(z, 0, "e4m3")))
    return s[:, unstriped(n4)] * f64(tab)[:, unstriped(n2)] + f64(tab)[:, unstriped(n3)]

@@ -1,0 +1,222 @@
+from contextlib import ExitStack
+
+import concourse.mybir as mybir
+
+K, T, S, H, C, J = 512, 2048, 512, 512, 512, 512
+FLOPS = 2 * K * H * S + 2 * K * C * S
+
+F32 = mybir.dt.float32
+BF16 = mybir.dt.bfloat16
+I32 = mybir.dt.int32
+U32 = mybir.dt.uint32
+U16 = mybir.dt.uint16
+U8 = mybir.dt.uint8
+FP8X4 = mybir.dt.float8_e4m3fn_x4
+ALU = mybir.AluOpType
+ACT = mybir.ActivationFunctionType
+
+P = 128
+PACK = 4
+GROUP = 16
+MEMBERS = 4
+Y_WINDOW = 1024
+S_WINDOW = 544
+GATHER = 512
+
+
+def tile_picked_hcandegpkinda_none_p_kernel(
+    tc, x_words, x_scales, w1, tau, gs, tab, offs, n1, cand, n2, n3, n4, out
+):
+    nc = tc.nc
+    with ExitStack() as ctx:
+        keep = ctx.enter_context(tc.tile_pool(name="keep", bufs=1))
+        shared = ctx.enter_context(tc.tile_pool(name="shared", bufs=1))
+        psum = ctx.enter_context(tc.psum_pool(name="psum", bufs=1))
+
+        def load_list(src, name):
+            lst = keep.tile(list(src.shape), U16, name=name)
+            nc.sync.dma_start(lst[:], src)
+            return lst
+
+        scale_table = keep.tile([P, T], U8, name="scale_table")
+        nc.gpsimd.memset(scale_table[:].bitcast(I32), 0)
+        offs_t = load_list(offs, "offs_t")
+        cand_t = load_list(cand, "cand_t")
+        scale_rows = x_scales[0].rearrange("(r e) c -> e r c", e=2)
+        for e in range(2):
+            nc.scalar.dma_start(scale_table[e:P:GROUP, :].bitcast(I32), scale_rows[e].bitcast(I32))
+        word_table = keep.tile([P, T], U32, name="word_table")
+        nc.sync.dma_start(word_table[:].bitcast(I32), x_words[0].rearrange("p n t -> p (n t)").bitcast(I32))
+        half = H // 2
+        w_rows = w1.rearrange("(p j) c -> p j c", j=PACK)
+        w_raw = []
+        for h in range(2):
+            raw = keep.tile([P, PACK, half], F32, name="w_raw%d" % h)
+            nc.sync.dma_start(raw[:], w_rows[:, :, h * half : (h + 1) * half])
+            w_raw.append(raw)
+        tau_t = keep.tile([P, PACK], F32, name="tau_t")
+        gs_t = keep.tile([P, PACK], F32, name="gs_t")
+        nc.gpsimd.dma_start(tau_t[:], tau.rearrange("(p t) o -> p (t o)", t=PACK))
+        nc.gpsimd.dma_start(gs_t[:], gs.rearrange("(p t) o -> p (t o)", t=PACK))
+        n1_t = load_list(n1, "n1_t")
+        n2_t = load_list(n2, "n2_t")
+        n3_t = load_list(n3, "n3_t")
+        n4_t = load_list(n4, "n4_t")
+
+        neg_tau = keep.tile([P, PACK], F32, name="neg_tau")
+        nc.scalar.activation(neg_tau[:], tau_t[:], ACT.Copy, scale=-1.0)
+        y_win = []
+        s_win = []
+        for t in range(PACK):
+            yw = keep.tile([P, Y_WINDOW], F32, name="y_win%d" % t)
+            nc.vector.memset(yw[:, S:], 0.0)
+            y_win.append(yw)
+            sw = keep.tile([P, S_WINDOW], F32, name="s_win%d" % t)
+            nc.gpsimd.memset(sw[:, S:], 0.0)
+            s_win.append(sw)
+
+        def pick_scales(lst, name):
+            picked = keep.tile([P, S], U8, name=name + "_picked")
+            nc.vector.tensor_copy(picked[:], scale_table[:].indirect(lst[:]))
+            plane = keep.tile([P, S], U8, name=name + "_plane", align_bytes=64)
+            nc.vector.tensor_copy(plane[:].bitcast(I32), picked[:].bitcast(I32))
+            for e in range(2):
+                nc.sync.dma_start(
+                    plane[2 + e : P : 2 * GROUP, :].bitcast(I32),
+                    picked[GROUP + e : P : 2 * GROUP, :].bitcast(I32),
+                )
+            return plane
+
+        def pick_words(lst, name):
+            words = keep.tile([P, S], U32, name=name, align_bytes=64)
+            nc.vector.tensor_copy(words[:], word_table[:].indirect(lst[:]))
+            return words
+
+        xq_scales = pick_scales(offs_t, "xq_scales")
+        xq_words = pick_words(offs_t, "xq_words")
+
+        w_bf = keep.tile([P, PACK * H], BF16, name="w_bf", align_bytes=64)
+        w_dealt = w_bf[:].rearrange("p (t m j) -> p m j t", t=PACK, j=PACK)
+        for h in range(2):
+            nc.scalar.copy(
+                w_dealt[:, h * (P // 2) : (h + 1) * (P // 2)],
+                w_raw[h][:].rearrange("p j (m t) -> p m j t", t=PACK),
+            )
+        w_codes = keep.tile([P, H], U32, name="w_codes", align_bytes=64)
+        w_scales = keep.tile([P, H], U8, name="w_scales", align_bytes=64)
+        y_bank = []
+        for t in range(PACK):
+            cols = slice(t * P, (t + 1) * P)
+            nc.vector.quantize_mx(
+                out=w_codes[:, cols].bitcast(FP8X4), scales=w_scales[:, cols], in_=w_bf[:, t * H : (t + 1) * H]
+            )
+            bank = psum.tile([P, S], F32, name="y_bank%d" % t, tag="y_bank%d" % t)
+            nc.tensor.matmul_mx(
+                out=bank[:],
+                lhsT=w_codes[:, cols].bitcast(FP8X4),
+                lhsT_scale=w_scales[:, cols],
+                rhs=xq_words[:].bitcast(FP8X4),
+                rhs_scale=xq_scales[:],
+                start=True,
+                stop=True,
+            )
+            y_bank.append(bank)
+
+        xc_scales = pick_scales(cand_t, "xc_scales")
+        xc_words = pick_words(cand_t, "xc_words")
+
+        top = keep.tile([P, PACK], F32, name="top")
+        bias = keep.tile([P, PACK], F32, name="bias")
+        u = keep.tile([P, PACK, S], F32, name="u")
+        for t in range(PACK):
+            col = slice(t, t + 1)
+            nc.vector.tensor_scalar(
+                y_win[t][:, :S], y_bank[t][:], 1.0, None, ALU.mult, ALU.max, accum_out=top[:, col]
+            )
+            nc.scalar.activation(bias[:, col], top[:, col], ACT.Copy, scale=neg_tau[:, col])
+            nc.gpsimd.tensor_scalar(u[:, t, :], y_win[t][:, :S], gs_t[:, col], 3.0, ALU.mult, ALU.mult)
+
+        step = GATHER // MEMBERS
+        early = 3 * step
+        s_bank = [psum.tile([P, early], F32, name="s_bank%d" % b) for b in range(PACK)]
+        s_last = psum.tile([P, PACK, step], F32, name="s_last", tag="y_bank0")
+        rounds = [
+            (0, 2 * step, [[(t, 0), (t, step)] for t in range(PACK)]),
+            (2 * step, step, [[(t, 2 * step), (t + 1, 2 * step)] for t in (0, 2)]),
+            (3 * step, step, [[(t, 3 * step), (t + 1, 3 * step)] for t in (0, 2)]),
+        ]
+        for r, (j0, width, units) in enumerate(rounds):
+            spread = keep.tile([P, PACK * width], F32, name="spread%d" % r)
+            for n, unit in enumerate(units):
+                name = "%d_%d" % (r, n)
+                if r == 1:
+                    ea = shared.tile([P, 2 * step, MEMBERS], F32, name="ea" + name, offset=n * 2 * GATHER * 4)
+                else:
+                    ea = keep.tile([P, 2 * step, MEMBERS], F32, name="ea" + name)
+                for g, (t, j) in enumerate(unit):
+                    nc.scalar.activation(
+                        ea[:, g * step : (g + 1) * step, :].rearrange("p j m -> p (j m)"),
+                        y_win[t][:].indirect(n1_t[:, j * MEMBERS // GROUP : (j + step) * MEMBERS // GROUP]),
+                        ACT.Exp,
+                        bias=bias[:, t : t + 1],
+                        scale=tau_t[:, t : t + 1],
+                    )
+                if (r, n) == (1, 1):
+                    hi = shared.tile([P, 2 * step, 2], F32, name="hi" + name, offset=4 * GATHER * 4)
+                else:
+                    hi = keep.tile([P, 2 * step, 2], F32, name="hi" + name)
+                lo = keep.tile([P, 2 * step, 2], F32, name="lo" + name)
+                mx = keep.tile([P, 2 * step], F32, name="mx" + name)
+                mn = keep.tile([P, 2 * step], F32, name="mn" + name)
+                nc.vector.tensor_tensor(hi[:], ea[:, :, 0:2], ea[:, :, 2:4], ALU.max)
+                nc.vector.tensor_tensor(lo[:], ea[:, :, 0:2], ea[:, :, 2:4], ALU.min)
+                nc.vector.tensor_tensor(mx[:], hi[:, :, 0], hi[:, :, 1], ALU.max)
+                nc.vector.tensor_tensor(mn[:], lo[:, :, 0], lo[:, :, 1], ALU.min)
+                nc.vector.tensor_tensor(spread[:, n * 2 * step : (n + 1) * 2 * step], mx[:], mn[:], ALU.subtract)
+            z_bf = keep.tile([P, PACK * width], BF16, name="z_bf%d" % r, align_bytes=64)
+            nc.vector.tensor_tensor(
+                z_bf[:].rearrange("p (c i t) -> p c t i", i=4, t=PACK),
+                spread[:].rearrange("p (t c i) -> p c t i", t=PACK, i=4),
+                u[:, :, j0 : j0 + width].rearrange("p t (c i) -> p c t i", i=4),
+                ALU.mult,
+            )
+            z_codes = keep.tile([P, width], U32, name="z_codes%d" % r, align_bytes=64)
+            z_scales = keep.tile([P, width], U8, name="z_scales%d" % r, align_bytes=64)
+            nc.vector.quantize_mx(out=z_codes[:].bitcast(FP8X4), scales=z_scales[:], in_=z_bf[:])
+            for b in range(PACK):
+                cols = slice(b * P, (b + 1) * P)
+                nc.tensor.matmul_mx(
+                    out=s_bank[b][:, j0 : j0 + width] if j0 < early else s_last[:, b, :],
+                    lhsT=xc_words[:, cols].bitcast(FP8X4),
+                    lhsT_scale=xc_scales[:, cols],
+                    rhs=z_codes[:].bitcast(FP8X4),
+                    rhs_scale=z_scales[:],
+                    start=True,
+                    stop=True,
+                )
+
+            if j0 + width == early:
+                for b in range(PACK):
+                    nc.scalar.activation(s_win[b][:, :early], s_bank[b][:], ACT.Copy, scale=0.0625)
+
+        tab_t = []
+        for b, place in enumerate((0, 2, 3, 4)):
+            tb = shared.tile([P, J], F32, name="tab%d" % b, offset=place * J * 4)
+            nc.sync.dma_start(tb[:], tab[b * P : (b + 1) * P, :])
+            tab_t.append(tb)
+        for b in range(PACK):
+            factor = keep.tile([P, S], F32, name="factor%d" % b)
+            term = keep.tile([P, S], F32, name="term%d" % b)
+            for dst, lst in ((factor, n2_t), (term, n3_t)):
+                for h in range(2):
+                    nc.scalar.activation(
+                        dst[:, h * half : (h + 1) * half],
+                        tab_t[b][:].indirect(lst[:, h * half // GROUP : (h + 1) * half // GROUP]),
+                        ACT.Copy,
+                    )
+            nc.vector.tensor_scalar(s_win[b][:, early:S], s_last[:, b, :], 0.0625, None, ALU.mult)
+            prod = keep.tile([P, S], F32, name="prod%d" % b)
+            nc.vector.tensor_tensor(prod[:], s_win[b][:].indirect(n4_t[:]), factor[:], ALU.mult)
+            res = keep.tile([P, S], F32, name="res%d" % b)
+            nc.vector.tensor_tensor(res[:], prod[:], term[:], ALU.add)
+            nc.sync.dma_start(out[b * P : (b + 1) * P, :], res[:])

@@ -39,12 +39,15 @@ def tile_picked_hcandegpkinda_none_p_kernel(
             return lst
 
         scale_table = keep.tile([P, T], U8, name="scale_table")
-        nc.gpsimd.memset(scale_table[:].bitcast(I32), 0)
+        nc.gpsimd.memset(scale_table[:, : T // 2].bitcast(I32), 0)
+        nc.vector.memset(scale_table[:, T // 2 :].bitcast(I32), 0)
         offs_t = load_list(offs, "offs_t")
         cand_t = load_list(cand, "cand_t")
-        scale_rows = x_scales[0].rearrange("(r e) c -> e r c", e=2)
-        for e in range(2):
-            nc.scalar.dma_start(scale_table[e:P:GROUP, :].bitcast(I32), scale_rows[e].bitcast(I32))
+        n1_t = load_list(n1, "n1_t")
+        n2_t = load_list(n2, "n2_t")
+        n3_t = load_list(n3, "n3_t")
+        n4_t = load_list(n4, "n4_t")
+        nc.sync.dma_start(scale_table[0:P:8, :].bitcast(I32), x_scales[0].bitcast(I32))
         word_table = keep.tile([P, T], U32, name="word_table")
         nc.sync.dma_start(word_table[:].bitcast(I32), x_words[0].rearrange("p n t -> p (n t)").bitcast(I32))
         half = H // 2
@@ -58,13 +61,14 @@ def tile_picked_hcandegpkinda_none_p_kernel(
         gs_t = keep.tile([P, PACK], F32, name="gs_t")
         nc.gpsimd.dma_start(tau_t[:], tau.rearrange("(p t) o -> p (t o)", t=PACK))
         nc.gpsimd.dma_start(gs_t[:], gs.rearrange("(p t) o -> p (t o)", t=PACK))
-        n1_t = load_list(n1, "n1_t")
-        n2_t = load_list(n2, "n2_t")
-        n3_t = load_list(n3, "n3_t")
-        n4_t = load_list(n4, "n4_t")
 
-        neg_tau = keep.tile([P, PACK], F32, name="neg_tau")
-        nc.scalar.activation(neg_tau[:], tau_t[:], ACT.Copy, scale=-1.0)
+        ea_bytes = 2 * GATHER * 4
+        cand_place = 3 * ea_bytes + PACK * J * 4
+        neg_a = shared.tile([P, PACK - 1], F32, name="neg_a", offset=cand_place, align_bytes=64)
+        neg_b = shared.tile([P, 1], F32, name="neg_b", offset=2 * ea_bytes)
+        nc.scalar.activation(neg_a[:], tau_t[:, : PACK - 1], ACT.Copy, scale=-1.0)
+        nc.scalar.activation(neg_b[:], tau_t[:, PACK - 1 :], ACT.Copy, scale=-1.0)
+        neg_tau = [neg_a[:, t : t + 1] for t in range(PACK - 1)] + [neg_b[:]]
         y_win = []
         s_win = []
         for t in range(PACK):
@@ -80,28 +84,26 @@ def tile_picked_hcandegpkinda_none_p_kernel(
             nc.vector.tensor_copy(picked[:], scale_table[:].indirect(lst[:]))
             plane = keep.tile([P, S], U8, name=name + "_plane", align_bytes=64)
             nc.vector.tensor_copy(plane[:].bitcast(I32), picked[:].bitcast(I32))
-            for e in range(2):
+            for e in range(1, 4):
                 nc.sync.dma_start(
-                    plane[2 + e : P : 2 * GROUP, :].bitcast(I32),
-                    picked[GROUP + e : P : 2 * GROUP, :].bitcast(I32),
+                    plane[e : P : 2 * GROUP, :].bitcast(I32),
+                    picked[8 * e : P : 2 * GROUP, :].bitcast(I32),
                 )
             return plane
 
-        def pick_words(lst, name):
-            words = keep.tile([P, S], U32, name=name, align_bytes=64)
+        def pick_words(lst, words):
             nc.vector.tensor_copy(words[:], word_table[:].indirect(lst[:]))
-            return words
 
         xq_scales = pick_scales(offs_t, "xq_scales")
-        xq_words = pick_words(offs_t, "xq_words")
+        xq_words = keep.tile([P, S], U32, name="xq_words", align_bytes=64)
+        pick_words(offs_t, xq_words)
 
         w_bf = keep.tile([P, PACK * H], BF16, name="w_bf", align_bytes=64)
         w_dealt = w_bf[:].rearrange("p (t m j) -> p m j t", t=PACK, j=PACK)
-        for h in range(2):
-            nc.scalar.copy(
-                w_dealt[:, h * (P // 2) : (h + 1) * (P // 2)],
-                w_raw[h][:].rearrange("p j (m t) -> p m j t", t=PACK),
-            )
+        w_src = [raw[:].rearrange("p j (m t) -> p m j t", t=PACK) for raw in w_raw]
+        nc.scalar.copy(w_dealt[:, 0:64], w_src[0])
+        nc.scalar.copy(w_dealt[:, 64:88], w_src[1][:, 0:24])
+        nc.vector.tensor_copy(w_dealt[:, 88:128], w_src[1][:, 24:64])
         w_codes = keep.tile([P, H], U32, name="w_codes", align_bytes=64)
         w_scales = keep.tile([P, H], U8, name="w_scales", align_bytes=64)
         y_bank = []
@@ -123,7 +125,6 @@ def tile_picked_hcandegpkinda_none_p_kernel(
             y_bank.append(bank)
 
         xc_scales = pick_scales(cand_t, "xc_scales")
-        xc_words = pick_words(cand_t, "xc_words")
 
         top = keep.tile([P, PACK], F32, name="top")
         bias = keep.tile([P, PACK], F32, name="bias")
@@ -133,60 +134,73 @@ def tile_picked_hcandegpkinda_none_p_kernel(
             nc.vector.tensor_scalar(
                 y_win[t][:, :S], y_bank[t][:], 1.0, None, ALU.mult, ALU.max, accum_out=top[:, col]
             )
-            nc.scalar.activation(bias[:, col], top[:, col], ACT.Copy, scale=neg_tau[:, col])
+            nc.scalar.activation(bias[:, col], top[:, col], ACT.Copy, scale=neg_tau[t])
             nc.gpsimd.tensor_scalar(u[:, t, :], y_win[t][:, :S], gs_t[:, col], 3.0, ALU.mult, ALU.mult)
+
+        xc_words = shared.tile([P, C], U32, name="xc_words", offset=cand_place, align_bytes=64)
+        pick_words(cand_t, xc_words)
 
         step = GATHER // MEMBERS
         early = 3 * step
         s_bank = [psum.tile([P, early], F32, name="s_bank%d" % b) for b in range(PACK)]
         s_last = psum.tile([P, PACK, step], F32, name="s_last", tag="y_bank0")
-        rounds = [
-            (0, 2 * step, [[(t, 0), (t, step)] for t in range(PACK)]),
-            (2 * step, step, [[(t, 2 * step), (t + 1, 2 * step)] for t in (0, 2)]),
-            (3 * step, step, [[(t, 3 * step), (t + 1, 3 * step)] for t in (0, 2)]),
-        ]
-        for r, (j0, width, units) in enumerate(rounds):
-            spread = keep.tile([P, PACK * width], F32, name="spread%d" % r)
-            for n, unit in enumerate(units):
-                name = "%d_%d" % (r, n)
-                if r == 1:
-                    ea = shared.tile([P, 2 * step, MEMBERS], F32, name="ea" + name, offset=n * 2 * GATHER * 4)
+        tab_place = [3 * ea_bytes + b * J * 4 for b in range(PACK)]
+        unit = 0
+        for r in range(S // step):
+            j0 = r * step
+            z_codes = keep.tile([P, step], U32, name="z_codes%d" % r, align_bytes=64)
+            z_scales = keep.tile([P, step], U8, name="z_scales%d" % r, align_bytes=64)
+            parts = 1 if j0 < early else 2
+            width = step // parts
+            for part in range(parts):
+                j = j0 + part * width
+                if r == 2:
+                    spread = shared.tile([P, PACK * width], F32, name="spread%d" % j, offset=tab_place[3])
                 else:
-                    ea = keep.tile([P, 2 * step, MEMBERS], F32, name="ea" + name)
-                for g, (t, j) in enumerate(unit):
-                    nc.scalar.activation(
-                        ea[:, g * step : (g + 1) * step, :].rearrange("p j m -> p (j m)"),
-                        y_win[t][:].indirect(n1_t[:, j * MEMBERS // GROUP : (j + step) * MEMBERS // GROUP]),
-                        ACT.Exp,
-                        bias=bias[:, t : t + 1],
-                        scale=tau_t[:, t : t + 1],
+                    spread = keep.tile([P, PACK * width], F32, name="spread%d" % j)
+                for n in range(2):
+                    name = "%d_%d" % (j, n)
+                    ea = shared.tile([P, 2 * width, MEMBERS], F32, name="ea" + name, offset=unit % 3 * ea_bytes)
+                    unit = unit + 1
+                    for g in range(2):
+                        t = 2 * n + g
+                        nc.scalar.activation(
+                            ea[:, g * width : (g + 1) * width, :].rearrange("p j m -> p (j m)"),
+                            y_win[t][:].indirect(n1_t[:, j * MEMBERS // GROUP : (j + width) * MEMBERS // GROUP]),
+                            ACT.Exp,
+                            bias=bias[:, t : t + 1],
+                            scale=tau_t[:, t : t + 1],
+                        )
+                    if r == 2:
+                        hi = shared.tile([P, 2 * width, 2], F32, name="hi" + name, offset=tab_place[n])
+                    else:
+                        hi = keep.tile([P, 2 * width, 2], F32, name="hi" + name)
+                    if (r, n) == (2, 1):
+                        lo = shared.tile([P, 2 * width, 2], F32, name="lo" + name, offset=tab_place[2])
+                    else:
+                        lo = keep.tile([P, 2 * width, 2], F32, name="lo" + name)
+                    mx = keep.tile([P, 2 * width], F32, name="mx" + name)
+                    mn = keep.tile([P, 2 * width], F32, name="mn" + name)
+                    nc.vector.tensor_tensor(hi[:], ea[:, :, 0:2], ea[:, :, 2:4], ALU.max)
+                    nc.vector.tensor_tensor(lo[:], ea[:, :, 0:2], ea[:, :, 2:4], ALU.min)
+                    nc.vector.tensor_tensor(mx[:], hi[:, :, 0], hi[:, :, 1], ALU.max)
+                    nc.vector.tensor_tensor(mn[:], lo[:, :, 0], lo[:, :, 1], ALU.min)
+                    nc.vector.tensor_tensor(
+                        spread[:, n * 2 * width : (n + 1) * 2 * width], mx[:], mn[:], ALU.subtract
                     )
-                if (r, n) == (1, 1):
-                    hi = shared.tile([P, 2 * step, 2], F32, name="hi" + name, offset=4 * GATHER * 4)
-                else:
-                    hi = keep.tile([P, 2 * step, 2], F32, name="hi" + name)
-                lo = keep.tile([P, 2 * step, 2], F32, name="lo" + name)
-                mx = keep.tile([P, 2 * step], F32, name="mx" + name)
-                mn = keep.tile([P, 2 * step], F32, name="mn" + name)
-                nc.vector.tensor_tensor(hi[:], ea[:, :, 0:2], ea[:, :, 2:4], ALU.max)
-                nc.vector.tensor_tensor(lo[:], ea[:, :, 0:2], ea[:, :, 2:4], ALU.min)
-                nc.vector.tensor_tensor(mx[:], hi[:, :, 0], hi[:, :, 1], ALU.max)
-                nc.vector.tensor_tensor(mn[:], lo[:, :, 0], lo[:, :, 1], ALU.min)
-                nc.vector.tensor_tensor(spread[:, n * 2 * step : (n + 1) * 2 * step], mx[:], mn[:], ALU.subtract)
-            z_bf = keep.tile([P, PACK * width], BF16, name="z_bf%d" % r, align_bytes=64)
-            nc.vector.tensor_tensor(
-                z_bf[:].rearrange("p (c i t) -> p c t i", i=4, t=PACK),
-                spread[:].rearrange("p (t c i) -> p c t i", t=PACK, i=4),
-                u[:, :, j0 : j0 + width].rearrange("p t (c i) -> p c t i", i=4),
-                ALU.mult,
-            )
-            z_codes = keep.tile([P, width], U32, name="z_codes%d" % r, align_bytes=64)
-            z_scales = keep.tile([P, width], U8, name="z_scales%d" % r, align_bytes=64)
-            nc.vector.quantize_mx(out=z_codes[:].bitcast(FP8X4), scales=z_scales[:], in_=z_bf[:])
+                z_bf = keep.tile([P, PACK * width], BF16, name="z_bf%d" % j, align_bytes=64)
+                nc.vector.tensor_tensor(
+                    z_bf[:].rearrange("p (c i t) -> p c t i", i=4, t=PACK),
+                    spread[:].rearrange("p (t c i) -> p c t i", t=PACK, i=4),
+                    u[:, :, j : j + width].rearrange("p t (c i) -> p c t i", i=4),
+                    ALU.mult,
+                )
+                cols = slice(part * width, (part + 1) * width)
+                nc.vector.quantize_mx(out=z_codes[:, cols].bitcast(FP8X4), scales=z_scales[:, cols], in_=z_bf[:])
             for b in range(PACK):
                 cols = slice(b * P, (b + 1) * P)
                 nc.tensor.matmul_mx(
-                    out=s_bank[b][:, j0 : j0 + width] if j0 < early else s_last[:, b, :],
+                    out=s_bank[b][:, j0 : j0 + step] if j0 < early else s_last[:, b, :],
                     lhsT=xc_words[:, cols].bitcast(FP8X4),
                     lhsT_scale=xc_scales[:, cols],
                     rhs=z_codes[:].bitcast(FP8X4),
@@ -194,14 +208,13 @@ def tile_picked_hcandegpkinda_none_p_kernel(
                     start=True,
                     stop=True,
                 )
-
-            if j0 + width == early:
+            if j0 + step == early:
                 for b in range(PACK):
                     nc.scalar.activation(s_win[b][:, :early], s_bank[b][:], ACT.Copy, scale=0.0625)
 
         tab_t = []
-        for b, place in enumerate((0, 2, 3, 4)):
-            tb = shared.tile([P, J], F32, name="tab%d" % b, offset=place * J * 4)
+        for b in range(PACK):
+            tb = shared.tile([P, J], F32, name="tab%d" % b, offset=tab_place[b])
             nc.sync.dma_start(tb[:], tab[b * P : (b + 1) * P, :])
             tab_t.append(tb)
         for b in range(PACK):
@@ -218,5 +231,8 @@ def tile_picked_hcandegpkinda_none_p_kernel(
             prod = keep.tile([P, S], F32, name="prod%d" % b)
             nc.vector.tensor_tensor(prod[:], s_win[b][:].indirect(n4_t[:]), factor[:], ALU.mult)
             res = keep.tile([P, S], F32, name="res%d" % b)
-            nc.vector.tensor_tensor(res[:], prod[:], term[:], ALU.add)
-            nc.sync.dma_start(out[b * P : (b + 1) * P, :], res[:])
+            pieces = 2 if b == PACK - 1 else 1
+            for h in range(pieces):
+                cols = slice(h * S // pieces, (h + 1) * S // pieces)
+                nc.vector.tensor_tensor(res[:, cols], prod[:, cols], term[:, cols], ALU.add)
+                nc.sync.dma_start(out[b * P : (b + 1) * P, cols], res[:, cols])

@@ -41,12 +41,14 @@ def tile_picked_hcandegpkinda_none_p_kernel(
         scale_table = keep.tile([P, T], U8, name="scale_table")
         nc.gpsimd.memset(scale_table[:, : T // 2].bitcast(I32), 0)
         nc.vector.memset(scale_table[:, T // 2 :].bitcast(I32), 0)
+        tau_t = keep.tile([P, PACK], F32, name="tau_t")
+        nc.sync.dma_start(tau_t[:], tau.rearrange("(p t) o -> p (t o)", t=PACK))
         offs_t = load_list(offs, "offs_t")
         cand_t = load_list(cand, "cand_t")
-        n1_t = load_list(n1, "n1_t")
+        tab_first = keep.tile([P, J], F32, name="tab0")
+        nc.sync.dma_start(tab_first[:], tab[0:P, :])
         n2_t = load_list(n2, "n2_t")
         n3_t = load_list(n3, "n3_t")
-        n4_t = load_list(n4, "n4_t")
         nc.sync.dma_start(scale_table[0:P:8, :].bitcast(I32), x_scales[0].bitcast(I32))
         word_table = keep.tile([P, T], U32, name="word_table")
         nc.sync.dma_start(word_table[:].bitcast(I32), x_words[0].rearrange("p n t -> p (n t)").bitcast(I32))
@@ -57,11 +59,11 @@ def tile_picked_hcandegpkinda_none_p_kernel(
             raw = keep.tile([P, PACK, half], F32, name="w_raw%d" % h)
             nc.sync.dma_start(raw[:], w_rows[:, :, h * half : (h + 1) * half])
             w_raw.append(raw)
-        tau_t = keep.tile([P, PACK], F32, name="tau_t")
         gs_t = keep.tile([P, PACK], F32, name="gs_t")
-        nc.gpsimd.dma_start(tau_t[:], tau.rearrange("(p t) o -> p (t o)", t=PACK))
         nc.gpsimd.dma_start(gs_t[:], gs.rearrange("(p t) o -> p (t o)", t=PACK))
 
+        n1_t = load_list(n1, "n1_t")
+        n4_t = load_list(n4, "n4_t")
         ea_bytes = 2 * GATHER * 4
         cand_place = 3 * ea_bytes + PACK * J * 4
         neg_a = shared.tile([P, PACK - 1], F32, name="neg_a", offset=cand_place, align_bytes=64)
@@ -69,11 +71,25 @@ def tile_picked_hcandegpkinda_none_p_kernel(
         nc.scalar.activation(neg_a[:], tau_t[:, : PACK - 1], ACT.Copy, scale=-1.0)
         nc.scalar.activation(neg_b[:], tau_t[:, PACK - 1 :], ACT.Copy, scale=-1.0)
         neg_tau = [neg_a[:, t : t + 1] for t in range(PACK - 1)] + [neg_b[:]]
+
+        def look_up_kinds(table, b):
+            factor = keep.tile([P, S], F32, name="factor%d" % b)
+            term = keep.tile([P, S], F32, name="term%d" % b)
+            for dst, lst in ((factor, n2_t), (term, n3_t)):
+                for h in range(2):
+                    nc.scalar.activation(
+                        dst[:, h * half : (h + 1) * half],
+                        table[:].indirect(lst[:, h * half // GROUP : (h + 1) * half // GROUP]),
+                        ACT.Copy,
+                    )
+            return factor, term
+
+        kinds = [look_up_kinds(tab_first, 0)]
         y_win = []
         s_win = []
         for t in range(PACK):
             yw = keep.tile([P, Y_WINDOW], F32, name="y_win%d" % t)
-            nc.vector.memset(yw[:, S:], 0.0)
+            (nc.vector if t < 2 else nc.gpsimd).memset(yw[:, S:], 0.0)
             y_win.append(yw)
             sw = keep.tile([P, S_WINDOW], F32, name="s_win%d" % t)
             nc.gpsimd.memset(sw[:, S:], 0.0)
@@ -143,18 +159,18 @@ def tile_picked_hcandegpkinda_none_p_kernel(
         step = GATHER // MEMBERS
         early = 3 * step
         s_bank = [psum.tile([P, early], F32, name="s_bank%d" % b) for b in range(PACK)]
-        s_last = psum.tile([P, PACK, step], F32, name="s_last", tag="y_bank0")
+        s_last = [psum.tile([P, step], F32, name="s_last%d" % b, tag="y_bank%d" % b) for b in range(PACK)]
         tab_place = [3 * ea_bytes + b * J * 4 for b in range(PACK)]
         unit = 0
         for r in range(S // step):
             j0 = r * step
             z_codes = keep.tile([P, step], U32, name="z_codes%d" % r, align_bytes=64)
             z_scales = keep.tile([P, step], U8, name="z_scales%d" % r, align_bytes=64)
-            parts = 1 if j0 < early else 2
+            parts = 1
             width = step // parts
             for part in range(parts):
                 j = j0 + part * width
-                if r == 2:
+                if r == 3:
                     spread = shared.tile([P, PACK * width], F32, name="spread%d" % j, offset=tab_place[3])
                 else:
                     spread = keep.tile([P, PACK * width], F32, name="spread%d" % j)
@@ -171,11 +187,11 @@ def tile_picked_hcandegpkinda_none_p_kernel(
                             bias=bias[:, t : t + 1],
                             scale=tau_t[:, t : t + 1],
                         )
-                    if r == 2:
-                        hi = shared.tile([P, 2 * width, 2], F32, name="hi" + name, offset=tab_place[n])
+                    if (r, n) == (2, 0):
+                        hi = shared.tile([P, 2 * width, 2], F32, name="hi" + name, offset=tab_place[1])
                     else:
                         hi = keep.tile([P, 2 * width, 2], F32, name="hi" + name)
-                    if (r, n) == (2, 1):
+                    if (r, n) == (3, 1):
                         lo = shared.tile([P, 2 * width, 2], F32, name="lo" + name, offset=tab_place[2])
                     else:
                         lo = keep.tile([P, 2 * width, 2], F32, name="lo" + name)
@@ -190,9 +206,9 @@ def tile_picked_hcandegpkinda_none_p_kernel(
                     )
                 z_bf = keep.tile([P, PACK * width], BF16, name="z_bf%d" % j, align_bytes=64)
                 nc.vector.tensor_tensor(
-                    z_bf[:].rearrange("p (c i t) -> p c t i", i=4, t=PACK),
-                    spread[:].rearrange("p (t c i) -> p c t i", t=PACK, i=4),
-                    u[:, :, j : j + width].rearrange("p t (c i) -> p c t i", i=4),
+                    z_bf[:].rearrange("p (c i t) -> p c t i", i=2, t=PACK),
+                    spread[:].rearrange("p (t c i) -> p c t i", t=PACK, i=2),
+                    u[:, :, j : j + width].rearrange("p t (c i) -> p c t i", i=2),
                     ALU.mult,
                 )
                 cols = slice(part * width, (part + 1) * width)
@@ -200,7 +216,7 @@ def tile_picked_hcandegpkinda_none_p_kernel(
             for b in range(PACK):
                 cols = slice(b * P, (b + 1) * P)
                 nc.tensor.matmul_mx(
-                    out=s_bank[b][:, j0 : j0 + step] if j0 < early else s_last[:, b, :],
+                    out=s_bank[b][:, j0 : j0 + step] if j0 < early else s_last[b][:],
                     lhsT=xc_words[:, cols].bitcast(FP8X4),
                     lhsT_scale=xc_scales[:, cols],
                     rhs=z_codes[:].bitcast(FP8X4),
@@ -212,22 +228,15 @@ def tile_picked_hcandegpkinda_none_p_kernel(
                 for b in range(PACK):
                     nc.scalar.activation(s_win[b][:, :early], s_bank[b][:], ACT.Copy, scale=0.0625)
 
-        tab_t = []
         for b in range(PACK):
+            nc.scalar.activation(s_win[b][:, early:S], s_last[b][:], ACT.Copy, scale=0.0625)
+
+        for b in range(1, PACK):
             tb = shared.tile([P, J], F32, name="tab%d" % b, offset=tab_place[b])
             nc.sync.dma_start(tb[:], tab[b * P : (b + 1) * P, :])
-            tab_t.append(tb)
+            kinds.append(look_up_kinds(tb, b))
         for b in range(PACK):
-            factor = keep.tile([P, S], F32, name="factor%d" % b)
-            term = keep.tile([P, S], F32, name="term%d" % b)
-            for dst, lst in ((factor, n2_t), (term, n3_t)):
-                for h in range(2):
-                    nc.scalar.activation(
-                        dst[:, h * half : (h + 1) * half],
-                        tab_t[b][:].indirect(lst[:, h * half // GROUP : (h + 1) * half // GROUP]),
-                        ACT.Copy,
-                    )
-            nc.vector.tensor_scalar(s_win[b][:, early:S], s_last[:, b, :], 0.0625, None, ALU.mult)
+            factor, term = kinds[b]
             prod = keep.tile([P, S], F32, name="prod%d" % b)
             nc.vector.tensor_tensor(prod[:], s_win[b][:].indirect(n4_t[:]), factor[:], ALU.mult)
             res = keep.tile([P, S], F32, name="res%d" % b)

@@ -95,13 +95,13 @@ def tile_picked_hcandegpkinda_none_p_kernel(
             nc.gpsimd.memset(sw[:, S:], 0.0)
             s_win.append(sw)
 
-        def pick_scales(lst, name):
+        def pick_scales(lst, name, queue):
             picked = keep.tile([P, S], U8, name=name + "_picked")
             nc.vector.tensor_copy(picked[:], scale_table[:].indirect(lst[:]))
             plane = keep.tile([P, S], U8, name=name + "_plane", align_bytes=64)
             nc.vector.tensor_copy(plane[:].bitcast(I32), picked[:].bitcast(I32))
             for e in range(1, 4):
-                nc.sync.dma_start(
+                queue.dma_start(
                     plane[e : P : 2 * GROUP, :].bitcast(I32),
                     picked[8 * e : P : 2 * GROUP, :].bitcast(I32),
                 )
@@ -110,7 +110,7 @@ def tile_picked_hcandegpkinda_none_p_kernel(
         def pick_words(lst, words):
             nc.vector.tensor_copy(words[:], word_table[:].indirect(lst[:]))
 
-        xq_scales = pick_scales(offs_t, "xq_scales")
+        xq_scales = pick_scales(offs_t, "xq_scales", nc.scalar)
         xq_words = keep.tile([P, S], U32, name="xq_words", align_bytes=64)
         pick_words(offs_t, xq_words)
 
@@ -140,7 +140,7 @@ def tile_picked_hcandegpkinda_none_p_kernel(
             )
             y_bank.append(bank)
 
-        xc_scales = pick_scales(cand_t, "xc_scales")
+        xc_scales = pick_scales(cand_t, "xc_scales", nc.sync)
 
         top = keep.tile([P, PACK], F32, name="top")
         bias = keep.tile([P, PACK], F32, name="bias")
@@ -150,7 +150,7 @@ def tile_picked_hcandegpkinda_none_p_kernel(
             nc.vector.tensor_scalar(
                 y_win[t][:, :S], y_bank[t][:], 1.0, None, ALU.mult, ALU.max, accum_out=top[:, col]
             )
-            nc.scalar.activation(bias[:, col], top[:, col], ACT.Copy, scale=neg_tau[t])
+            nc.vector.tensor_scalar(bias[:, col], top[:, col], neg_tau[t], None, ALU.mult)
             nc.gpsimd.tensor_scalar(u[:, t, :], y_win[t][:, :S], gs_t[:, col], 3.0, ALU.mult, ALU.mult)
 
         xc_words = shared.tile([P, C], U32, name="xc_words", offset=cand_place, align_bytes=64)
@@ -166,14 +166,11 @@ def tile_picked_hcandegpkinda_none_p_kernel(
             j0 = r * step
             z_codes = keep.tile([P, step], U32, name="z_codes%d" % r, align_bytes=64)
             z_scales = keep.tile([P, step], U8, name="z_scales%d" % r, align_bytes=64)
-            parts = 1
+            parts = 1 if j0 < early else 2
             width = step // parts
             for part in range(parts):
                 j = j0 + part * width
-                if r == 3:
-                    spread = shared.tile([P, PACK * width], F32, name="spread%d" % j, offset=tab_place[3])
-                else:
-                    spread = keep.tile([P, PACK * width], F32, name="spread%d" % j)
+                spread = keep.tile([P, PACK * width], F32, name="spread%d" % j)
                 for n in range(2):
                     name = "%d_%d" % (j, n)
                     ea = shared.tile([P, 2 * width, MEMBERS], F32, name="ea" + name, offset=unit % 3 * ea_bytes)
@@ -191,8 +188,8 @@ def tile_picked_hcandegpkinda_none_p_kernel(
                         hi = shared.tile([P, 2 * width, 2], F32, name="hi" + name, offset=tab_place[1])
                     else:
                         hi = keep.tile([P, 2 * width, 2], F32, name="hi" + name)
-                    if (r, n) == (3, 1):
-                        lo = shared.tile([P, 2 * width, 2], F32, name="lo" + name, offset=tab_place[2])
+                    if j == S - width:
+                        lo = shared.tile([P, 2 * width, 2], F32, name="lo" + name, offset=tab_place[2 + n])
                     else:
                         lo = keep.tile([P, 2 * width, 2], F32, name="lo" + name)
                     mx = keep.tile([P, 2 * width], F32, name="mx" + name)

from contextlib import ExitStack

import concourse.mybir as mybir

K, T, S, H, C, J = 512, 2048, 512, 512, 512, 512
FLOPS = 2 * K * H * S + 2 * K * C * S

F32 = mybir.dt.float32
BF16 = mybir.dt.bfloat16
I32 = mybir.dt.int32
U32 = mybir.dt.uint32
U16 = mybir.dt.uint16
U8 = mybir.dt.uint8
FP8X4 = mybir.dt.float8_e4m3fn_x4
ALU = mybir.AluOpType
ACT = mybir.ActivationFunctionType

P = 128
PACK = 4
GROUP = 16
MEMBERS = 4
Y_WINDOW = 1024
S_WINDOW = 544
GATHER = 512


def tile_picked_hcandegpkinda_none_p_kernel(
    tc, x_words, x_scales, w1, tau, gs, tab, offs, n1, cand, n2, n3, n4, out
):
    nc = tc.nc
    with ExitStack() as ctx:
        keep = ctx.enter_context(tc.tile_pool(name="keep", bufs=1))
        shared = ctx.enter_context(tc.tile_pool(name="shared", bufs=1))
        psum = ctx.enter_context(tc.psum_pool(name="psum", bufs=1))

        def load_list(src, name):
            lst = keep.tile(list(src.shape), U16, name=name)
            nc.sync.dma_start(lst[:], src)
            return lst

        scale_table = keep.tile([P, T], U8, name="scale_table")
        nc.gpsimd.memset(scale_table[:, : T // 2].bitcast(I32), 0)
        nc.vector.memset(scale_table[:, T // 2 :].bitcast(I32), 0)
        tau_t = keep.tile([P, PACK], F32, name="tau_t")
        nc.sync.dma_start(tau_t[:], tau.rearrange("(p t) o -> p (t o)", t=PACK))
        offs_t = load_list(offs, "offs_t")
        cand_t = load_list(cand, "cand_t")
        tab_first = keep.tile([P, J], F32, name="tab0")
        nc.sync.dma_start(tab_first[:], tab[0:P, :])
        n2_t = load_list(n2, "n2_t")
        n3_t = load_list(n3, "n3_t")
        nc.sync.dma_start(scale_table[0:P:8, :].bitcast(I32), x_scales[0].bitcast(I32))
        word_table = keep.tile([P, T], U32, name="word_table")
        nc.sync.dma_start(word_table[:].bitcast(I32), x_words[0].rearrange("p n t -> p (n t)").bitcast(I32))
        half = H // 2
        w_rows = w1.rearrange("(p j) c -> p j c", j=PACK)
        w_raw = []
        for h in range(2):
            raw = keep.tile([P, PACK, half], F32, name="w_raw%d" % h)
            nc.sync.dma_start(raw[:], w_rows[:, :, h * half : (h + 1) * half])
            w_raw.append(raw)
        gs_t = keep.tile([P, PACK], F32, name="gs_t")
        nc.gpsimd.dma_start(gs_t[:], gs.rearrange("(p t) o -> p (t o)", t=PACK))

        n1_t = load_list(n1, "n1_t")
        n4_t = load_list(n4, "n4_t")
        ea_bytes = 2 * GATHER * 4
        cand_place = 3 * ea_bytes + PACK * J * 4
        neg_a = shared.tile([P, PACK - 1], F32, name="neg_a", offset=cand_place, align_bytes=64)
        neg_b = shared.tile([P, 1], F32, name="neg_b", offset=2 * ea_bytes)
        nc.scalar.activation(neg_a[:], tau_t[:, : PACK - 1], ACT.Copy, scale=-1.0)
        nc.scalar.activation(neg_b[:], tau_t[:, PACK - 1 :], ACT.Copy, scale=-1.0)
        neg_tau = [neg_a[:, t : t + 1] for t in range(PACK - 1)] + [neg_b[:]]

        def look_up_kinds(table, b):
            factor = keep.tile([P, S], F32, name="factor%d" % b)
            term = keep.tile([P, S], F32, name="term%d" % b)
            for dst, lst in ((factor, n2_t), (term, n3_t)):
                for h in range(2):
                    nc.scalar.activation(
                        dst[:, h * half : (h + 1) * half],
                        table[:].indirect(lst[:, h * half // GROUP : (h + 1) * half // GROUP]),
                        ACT.Copy,
                    )
            return factor, term

        kinds = [look_up_kinds(tab_first, 0)]
        y_win = []
        s_win = []
        for t in range(PACK):
            yw = keep.tile([P, Y_WINDOW], F32, name="y_win%d" % t)
            (nc.vector if t < 2 else nc.gpsimd).memset(yw[:, S:], 0.0)
            y_win.append(yw)
            sw = keep.tile([P, S_WINDOW], F32, name="s_win%d" % t)
            nc.gpsimd.memset(sw[:, S:], 0.0)
            s_win.append(sw)

        def pick_scales(lst, name, queue):
            picked = keep.tile([P, S], U8, name=name + "_picked")
            nc.vector.tensor_copy(picked[:], scale_table[:].indirect(lst[:]))
            plane = keep.tile([P, S], U8, name=name + "_plane", align_bytes=64)
            nc.vector.tensor_copy(plane[:].bitcast(I32), picked[:].bitcast(I32))
            for e in range(1, 4):
                queue.dma_start(
                    plane[e : P : 2 * GROUP, :].bitcast(I32),
                    picked[8 * e : P : 2 * GROUP, :].bitcast(I32),
                )
            return plane

        def pick_words(lst, words):
            nc.vector.tensor_copy(words[:], word_table[:].indirect(lst[:]))

        xq_scales = pick_scales(offs_t, "xq_scales", nc.scalar)
        xq_words = keep.tile([P, S], U32, name="xq_words", align_bytes=64)
        pick_words(offs_t, xq_words)

        w_bf = keep.tile([P, PACK * H], BF16, name="w_bf", align_bytes=64)
        w_dealt = w_bf[:].rearrange("p (t m j) -> p m j t", t=PACK, j=PACK)
        w_src = [raw[:].rearrange("p j (m t) -> p m j t", t=PACK) for raw in w_raw]
        nc.scalar.copy(w_dealt[:, 0:64], w_src[0])
        nc.scalar.copy(w_dealt[:, 64:88], w_src[1][:, 0:24])
        nc.vector.tensor_copy(w_dealt[:, 88:128], w_src[1][:, 24:64])
        w_codes = keep.tile([P, H], U32, name="w_codes", align_bytes=64)
        w_scales = keep.tile([P, H], U8, name="w_scales", align_bytes=64)
        y_bank = []
        for t in range(PACK):
            cols = slice(t * P, (t + 1) * P)
            nc.vector.quantize_mx(
                out=w_codes[:, cols].bitcast(FP8X4), scales=w_scales[:, cols], in_=w_bf[:, t * H : (t + 1) * H]
            )
            bank = psum.tile([P, S], F32, name="y_bank%d" % t, tag="y_bank%d" % t)
            nc.tensor.matmul_mx(
                out=bank[:],
                lhsT=w_codes[:, cols].bitcast(FP8X4),
                lhsT_scale=w_scales[:, cols],
                rhs=xq_words[:].bitcast(FP8X4),
                rhs_scale=xq_scales[:],
                start=True,
                stop=True,
            )
            y_bank.append(bank)

        xc_scales = pick_scales(cand_t, "xc_scales", nc.sync)

        top = keep.tile([P, PACK], F32, name="top")
        bias = keep.tile([P, PACK], F32, name="bias")
        u = keep.tile([P, PACK, S], F32, name="u")
        for t in range(PACK):
            col = slice(t, t + 1)
            nc.vector.tensor_scalar(
                y_win[t][:, :S], y_bank[t][:], 1.0, None, ALU.mult, ALU.max, accum_out=top[:, col]
            )
            nc.vector.tensor_scalar(bias[:, col], top[:, col], neg_tau[t], None, ALU.mult)
            nc.gpsimd.tensor_scalar(u[:, t, :], y_win[t][:, :S], gs_t[:, col], 3.0, ALU.mult, ALU.mult)

        xc_words = shared.tile([P, C], U32, name="xc_words", offset=cand_place, align_bytes=64)
        pick_words(cand_t, xc_words)

        step = GATHER // MEMBERS
        early = 3 * step
        s_bank = [psum.tile([P, early], F32, name="s_bank%d" % b) for b in range(PACK)]
        s_last = [psum.tile([P, step], F32, name="s_last%d" % b, tag="y_bank%d" % b) for b in range(PACK)]
        tab_place = [3 * ea_bytes + b * J * 4 for b in range(PACK)]
        unit = 0
        for r in range(S // step):
            j0 = r * step
            z_codes = keep.tile([P, step], U32, name="z_codes%d" % r, align_bytes=64)
            z_scales = keep.tile([P, step], U8, name="z_scales%d" % r, align_bytes=64)
            parts = 1 if j0 < early else 2
            width = step // parts
            for part in range(parts):
                j = j0 + part * width
                spread = keep.tile([P, PACK * width], F32, name="spread%d" % j)
                for n in range(2):
                    name = "%d_%d" % (j, n)
                    ea = shared.tile([P, 2 * width, MEMBERS], F32, name="ea" + name, offset=unit % 3 * ea_bytes)
                    unit = unit + 1
                    for g in range(2):
                        t = 2 * n + g
                        nc.scalar.activation(
                            ea[:, g * width : (g + 1) * width, :].rearrange("p j m -> p (j m)"),
                            y_win[t][:].indirect(n1_t[:, j * MEMBERS // GROUP : (j + width) * MEMBERS // GROUP]),
                            ACT.Exp,
                            bias=bias[:, t : t + 1],
                            scale=tau_t[:, t : t + 1],
                        )
                    if (r, n) == (2, 0):
                        hi = shared.tile([P, 2 * width, 2], F32, name="hi" + name, offset=tab_place[1])
                    else:
                        hi = keep.tile([P, 2 * width, 2], F32, name="hi" + name)
                    if j == S - width:
                        lo = shared.tile([P, 2 * width, 2], F32, name="lo" + name, offset=tab_place[2 + n])
                    else:
                        lo = keep.tile([P, 2 * width, 2], F32, name="lo" + name)
                    mx = keep.tile([P, 2 * width], F32, name="mx" + name)
                    mn = keep.tile([P, 2 * width], F32, name="mn" + name)
                    nc.vector.tensor_tensor(hi[:], ea[:, :, 0:2], ea[:, :, 2:4], ALU.max)
                    nc.vector.tensor_tensor(lo[:], ea[:, :, 0:2], ea[:, :, 2:4], ALU.min)
                    nc.vector.tensor_tensor(mx[:], hi[:, :, 0], hi[:, :, 1], ALU.max)
                    nc.vector.tensor_tensor(mn[:], lo[:, :, 0], lo[:, :, 1], ALU.min)
                    nc.vector.tensor_tensor(
                        spread[:, n * 2 * width : (n + 1) * 2 * width], mx[:], mn[:], ALU.subtract
                    )
                z_bf = keep.tile([P, PACK * width], BF16, name="z_bf%d" % j, align_bytes=64)
                nc.vector.tensor_tensor(
                    z_bf[:].rearrange("p (c i t) -> p c t i", i=2, t=PACK),
                    spread[:].rearrange("p (t c i) -> p c t i", t=PACK, i=2),
                    u[:, :, j : j + width].rearrange("p t (c i) -> p c t i", i=2),
                    ALU.mult,
                )
                cols = slice(part * width, (part + 1) * width)
                nc.vector.quantize_mx(out=z_codes[:, cols].bitcast(FP8X4), scales=z_scales[:, cols], in_=z_bf[:])
            for b in range(PACK):
                cols = slice(b * P, (b + 1) * P)
                nc.tensor.matmul_mx(
                    out=s_bank[b][:, j0 : j0 + step] if j0 < early else s_last[b][:],
                    lhsT=xc_words[:, cols].bitcast(FP8X4),
                    lhsT_scale=xc_scales[:, cols],
                    rhs=z_codes[:].bitcast(FP8X4),
                    rhs_scale=z_scales[:],
                    start=True,
                    stop=True,
                )
            if j0 + step == early:
                for b in range(PACK):
                    nc.scalar.activation(s_win[b][:, :early], s_bank[b][:], ACT.Copy, scale=0.0625)

        for b in range(PACK):
            nc.scalar.activation(s_win[b][:, early:S], s_last[b][:], ACT.Copy, scale=0.0625)

        for b in range(1, PACK):
            tb = shared.tile([P, J], F32, name="tab%d" % b, offset=tab_place[b])
            nc.sync.dma_start(tb[:], tab[b * P : (b + 1) * P, :])
            kinds.append(look_up_kinds(tb, b))
        for b in range(PACK):
            factor, term = kinds[b]
            prod = keep.tile([P, S], F32, name="prod%d" % b)
            nc.vector.tensor_tensor(prod[:], s_win[b][:].indirect(n4_t[:]), factor[:], ALU.mult)
            res = keep.tile([P, S], F32, name="res%d" % b)
            pieces = 2 if b == PACK - 1 else 1
            for h in range(pieces):
                cols = slice(h * S // pieces, (h + 1) * S // pieces)
                nc.vector.tensor_tensor(res[:, cols], prod[:, cols], term[:, cols], ALU.add)
                nc.sync.dma_start(out[b * P : (b + 1) * P, cols], res[:, cols])
